import numpy as np, ml_dtypes
CORES = [3,5,43,45,51,53,67,69,75,77,83,85,91,93,115,117]
N = 16
import mx_ref
NC, D = 128, 2
SRC = [[1,13],[6,14],[5,10],[3,9],[2,14],[3,8],[7,11],[0,11],[1,12],[2,12],[3,14],[4,10],[2,12],[2,14],[6,15],[3,6]]
BF = ml_dtypes.bfloat16
def setup_inputs(rng):
    def f(*shape):
        return mx_ref.flush((rng.standard_normal(shape, dtype=np.float32) * np.exp2(rng.integers(-2, 3, shape[:-1] + (1,)))).astype(BF))
    return {"w": f(N, 128, D * 512), "x": f(N, 128, 4 * NC)}
def setup_inputs_blocks(rng):
    d = setup_inputs(rng)
    for k in ("w", "x"): d[k] = mx_ref.spread(d[k], rng, 1)
    return d
def setup_inputs_wide(rng):
    d = setup_inputs(rng)
    for k in ("w", "x"): d[k] = mx_ref.flush((d[k].astype(np.float32) * np.exp2(rng.integers(-8, 9, (N, 1, 1))).astype(np.float32)).astype(BF))
    return d
def setup_inputs_zeros(rng):
    d = setup_inputs(rng); v = d["x"].reshape(N, 128, -1, 4).copy()
    v[np.broadcast_to((rng.random((N, 1, v.shape[2], 1)) < 0.33), v.shape)] = 0
    d["x"] = v.reshape(d["x"].shape)
    return d
def reference(w, x):
    QX = [mx_ref.quantize(x[j]) for j in range(N)]
    y = np.zeros((N, 128, NC), np.float32)
    for r in range(N):
        for i in range(D):
            p = mx_ref.matmul(mx_ref.quantize(w[r][:, 512 * i:512 * i + 512]), QX[SRC[r][i]])
            y[r] = p if i == 0 else y[r] + p
    return {"y": y}

from concourse.bass import DstId, RemoteDMATransfer
from concourse.mybir import dt

NT = 16
NC = 128
MAX_DIRECT = 2
K_OFF = 8
K_ON = 16
K_FEED = 8

SCRATCH = {
    "xb": ("sbuf", [128, 4 * NC], "bfloat16"),
    "wb": ("sbuf", [128, 8 * NC], "bfloat16"),
    "xq": ("sbuf", [128, NC], "float8_e4m3fn_x4"),
    "xs": ("sbuf", [128, NC], "uint8"),
    "wq": ("sbuf", [128, 2 * NC], "float8_e4m3fn_x4"),
    "ws": ("sbuf", [128, 2 * NC], "uint8"),
    "lq0": ("sbuf", [128, NC], "float8_e4m3fn_x4"),
    "ls0": ("sbuf", [128, NC], "uint8"),
    "lq1": ("sbuf", [128, NC], "float8_e4m3fn_x4"),
    "ls1": ("sbuf", [128, NC], "uint8"),
    "acc": ("psum", [128, 512], "float32"),
    "yb": ("sbuf", [128, NC], "float32"),
}
SEMAPHORES = (["ldx", "ldw", "qx", "qw", "mm", "cp", "st", "snt"]
              + ["s%d" % j for j in range(NT)] + ["q%d" % j for j in range(NT)])

CACHE = {}


def bits(mask):
    return bin(mask).count("1")


def pick(mask, k):
    eng = [e for e in range(mask.bit_length()) if mask >> e & 1]
    return sum(1 << e for e in eng[::len(eng) // k][:k])


def hops(topo, a, b):
    ca, cb = topo.chip(a), topo.chip(b)
    if ca == cb:
        return 0
    return 1 if (topo.mates(ca, cb) or topo.same_plane(ca, cb)) else 2


def build_plan(cores, src, topo):
    n = len(cores)
    group = set(cores)
    every = range(topo.CHIPS * topo.CORES_PER_CHIP)
    want = [[cores[r] for r in range(n) if r != j and j in src[r]] for j in range(n)]
    load = dict((cores[j], len(want[j])) for j in range(n))
    taken = set()

    def idle_core(s, d):
        c = [h for h in every if topo.chip(h) == topo.chip(s) and h not in group and h not in taken
             and topo.may_write(h, d)]
        c.sort(key=lambda h: (topo.die(h) != topo.die(s), h))
        taken.add(c[0])
        return c[0]

    kids = []
    for j in range(n):
        s = cores[j]
        k = {s: []}
        near = [d for d in want[j] if topo.chip(d) == topo.chip(s)]
        far = {}
        for d in want[j]:
            if topo.chip(d) != topo.chip(s):
                far.setdefault(topo.chip(d), []).append(d)
        entries = []
        for ch in sorted(far):
            ds = sorted(far[ch], key=lambda d: (load[d], d))
            entries.append(ds[0])
            if ds[1:]:
                k[ds[0]] = ds[1:]
        direct = [e for e in entries if topo.may_write(s, e)]
        hand = []
        for e in entries:
            if e in direct:
                continue
            via = [d for d in near if topo.may_write(d, e) and d not in k]
            if via:
                k[via[0]] = [e]
            else:
                h = idle_core(s, e)
                hand.append(h)
                k[h] = [e]
        first = None
        if len(direct) > MAX_DIRECT:
            pairs = [(hops(topo, a, b) - hops(topo, s, b), hops(topo, a, b), a, b) for a in direct for b in direct
                     if a != b and b not in k and topo.may_write(a, b)]
            if pairs:
                first, b = min(pairs)[2:]
                k[first] = k.get(first, []) + [b]
                direct.remove(b)
        direct.sort(key=lambda e: (e != first, -len(k.get(e, [])), e))
        while len(direct) > MAX_DIRECT:
            b = direct.pop()
            h = idle_core(s, b)
            hand.append(h)
            k[h] = [b]
        k[s] = hand + near + direct
        kids.append(k)

    when = [dict() for _ in range(n)]
    for j in range(n):
        todo = [(cores[j], 0)]
        while todo:
            c, t = todo.pop()
            when[j][c] = t
            off = 0
            for d in kids[j].get(c, []):
                out = topo.chip(d) != topo.chip(c)
                todo.append((d, t + 2 + (off if out else 0) + (0 if c in group else 1)))
                off += 1 if out else 0

    calls, expect = {}, {}
    for c in every:
        mine = sorted([j for j in range(n) if kids[j].get(c)], key=lambda j: when[j][c])
        for j in mine:
            on = [d for d in kids[j][c] if topo.chip(d) == topo.chip(c)]
            off = [d for d in kids[j][c] if topo.chip(d) != topo.chip(c)]
            m_on = m_off = 0
            if off:
                m_off = pick(topo.mask(c, off[0]), K_OFF)
            if on and off:
                m_on = pick(topo.mask(c, on[0]) & ~topo.mask(c, off[0]), K_FEED)
            elif on:
                m_on = pick(topo.mask(c, on[0]), K_ON)
            head = ([(on, m_on)] if on else []) + ([(off[:1], m_off)] if off else [])
            seq = [("s", head), ("q", head)]
            for d in off[1:]:
                seq += [("s", [([d], m_off)]), ("q", [([d], m_off)])]
            for part, trs in seq:
                calls.setdefault(c, []).append((part, j, trs))
                for ds, m in trs:
                    for d in ds:
                        expect.setdefault(d, {})[(part, j)] = bits(m)
    return {"calls": calls, "expect": expect, "when": when, "kids": kids}


def rank_program(g, core, T, topo):
    src = T.tables["SRC"]
    if "plan" not in CACHE:
        CACHE["plan"] = build_plan(list(T.cores), src, topo)
    plan = CACHE["plan"]
    rank = T.rank_of(core)
    calls = plan["calls"].get(core, [])
    expect = plan["expect"].get(core, {})
    sem = T.sem
    if rank is None and not calls:
        return

    def slot(c, j):
        r = T.rank_of(c)
        return 0 if r is None else src[r].index(j)

    def view(part, c, j):
        if T.rank_of(c) == j:
            return T.xs[:] if part == "s" else T.xq[:].bitcast(dt.uint8)
        if part == "s":
            return T["ls%d" % slot(c, j)][:]
        return T["lq%d" % slot(c, j)][:].bitcast(dt.uint8)

    if rank is not None:
        g.sync.dma_start(T.xb[:], T.x[:]).then_inc(sem.ldx, 16)
        g.sync.dma_start(T.wb[:], T.w[:]).then_inc(sem.ldw, 16)
        g.vector.wait_ge(sem.ldx, 16)
        g.vector.quantize_mx(T.xq[:], T.xs[:], T.xb[:]).then_inc(sem.qx, 1)
        g.vector.wait_ge(sem.ldw, 16)
        g.vector.quantize_mx(T.wq[:], T.ws[:], T.wb[:]).then_inc(sem.qw, 1)
        g.wait_ge(sem.qx, 1)

    sent = 0
    seen = set()
    for part, j, trs in calls:
        if j != rank and (part, j) not in seen:
            seen.add((part, j))
            g.wait_ge(sem[part + str(j)], expect[(part, j)])
        batch = []
        for ds, m in trs:
            ids = []
            for d in ds:
                rid, pid = topo.addr(d)[:2]
                ids.append(DstId(rid=rid, pnc=pid))
            batch.append(RemoteDMATransfer(dst_ids=ids, dma_engine_mask=m, remote_sem=sem[part + str(j)],
                                           srcs=[view(part, core, j)], dsts=[view(part, d, j) for d in ds]))
            sent += bits(m)
        g.remote_dma_fused(batch, local_sem=sem.snt)
    if sent:
        g.wait_ge(sem.snt, sent)
    if rank is None:
        return

    order = sorted(range(len(src[rank])), key=lambda i: plan["when"][src[rank][i]][core])
    g.tensor.wait_ge(sem.qw, 1)
    last = None
    for k, i in enumerate(order):
        j = src[rank][i]
        if j == rank:
            g.tensor.wait_ge(sem.qx, 1)
            rq, rs = T.xq[:], T.xs[:]
        else:
            g.tensor.wait_ge(sem["s%d" % j], expect[("s", j)])
            g.tensor.wait_ge(sem["q%d" % j], expect[("q", j)])
            rq, rs = T["lq%d" % i][:], T["ls%d" % i][:]
        last = g.tensor.matmul_mx(T.acc[:, 0:NC], T.wq[:, NC * i:NC * (i + 1)], T.ws[:, NC * i:NC * (i + 1)],
                                  rq, rs, k == 0, k == len(order) - 1)
    last.then_inc(sem.mm, 1)
    g.vector.wait_ge(sem.mm, 1)
    g.vector.tensor_copy(T.yb[:], T.acc[:, 0:NC]).then_inc(sem.cp, 1)
    g.sync.wait_ge(sem.cp, 1)
    g.sync.dma_start(T.y[:], T.yb[:]).then_inc(sem.st, 16)
    g.sync.wait_ge(sem.st, 16)
